import numpy as np
CORES = [33,34,161,162,289,290,417,418]
N = 8
TK = 256
D = 128 * N
EPS = 0.01
def setup_inputs(rng):
    return {"x": (rng.standard_normal((N, 128, TK), dtype=np.float32) * (0.5 + np.abs(rng.standard_normal((1, 1, TK), dtype=np.float32))) + rng.standard_normal((1, 1, TK), dtype=np.float32))}
def setup_inputs_big(rng):
    d = setup_inputs(rng)
    for k in ("x",): d[k] = (d[k].astype(np.float32) * 1024.0).astype(d[k].dtype)
    return d
def setup_inputs_small(rng):
    d = setup_inputs(rng)
    for k in ("x",): d[k] = (d[k].astype(np.float32) * (1 / 1024.0)).astype(d[k].dtype)
    return d
def setup_inputs_apart(rng):
    d = setup_inputs(rng)
    f = (10.0 ** rng.permutation(np.linspace(-1.5, 1.5, N))).astype(np.float32).reshape(N, 1, 1)
    for k in ("x",): d[k] = (d[k].astype(np.float32) * f).astype(d[k].dtype)
    return d
def setup_inputs_mixed(rng):
    d = setup_inputs(rng)
    f = (10.0 ** rng.uniform(-3, 3, (1, 1, TK))).astype(np.float32); shape = rng.integers(3, size=(1, 1, TK))
    for k in ("x",):
        x = d[k].astype(np.float32)
        m = x.mean(axis=(0, 1), keepdims=True); level = m + np.sign(x - m) * np.abs(x - m).mean(axis=(0, 1), keepdims=True) * rng.uniform(0.9, 1.1, x.shape).astype(np.float32)
        other = x * np.where(rng.random(x.shape) < 0.5, 0.1, 1.0).astype(np.float32)
        d[k] = (np.where(shape == 1, level, np.where(shape == 2, other, x)) * f).astype(d[k].dtype)
    return d
def setup_inputs_offset(rng):
    d = setup_inputs(rng)
    x = d["x"]; spread = x.std(axis=(0, 1), keepdims=True)
    d["x"] = (x + spread * rng.uniform(16, 48, (1, 1, TK)) * rng.choice([-1.0, 1.0], (1, 1, TK))).astype(np.float32)
    return d
def reference(x):
    X = x.astype(np.float64)
    mu = X.sum(axis=(0, 1)) / D
    Z = X - mu
    Z = Z / np.sqrt((Z ** 2).sum(axis=(0, 1)) / D + EPS)
    return {"y": Z.astype(np.float32)}

@@ -1,0 +1,198 @@
+import math
+from concourse.bass import DstId, RemoteDMATransfer
+from concourse.mybir import AluOpType, AxisListType, ActivationFunctionType
+
+P = 128
+H = 64
+EPS = 0.01
+NENG = 8
+RACK_FIRST = True
+
+SCRATCH = {
+    "xs": ("sbuf", [P, 256], "float32"),
+    "cst": ("sbuf", [P, P], "float32"),
+    "idn": ("sbuf", [P, P], "float32"),
+    "st": ("sbuf", [P, 32], "float32"),
+    "j0": ("sbuf", [P, P], "float32"),
+    "j1": ("sbuf", [P, P], "float32"),
+    "j2": ("sbuf", [P, 8], "float32"),
+    "j3": ("sbuf", [P, 8], "float32"),
+    "sig": ("sbuf", [P, 2], "float32"),
+    "cc": ("sbuf", [P, 2], "float32"),
+    "sc": ("sbuf", [P, 2], "float32"),
+    "dg0": ("sbuf", [P, P], "float32"),
+    "dg1": ("sbuf", [P, P], "float32"),
+    "nsum": ("sbuf", [P, 2], "float32"),
+    "qsum": ("sbuf", [P, 2], "float32"),
+    "tq": ("sbuf", [P, 2], "float32"),
+    "dd": ("sbuf", [P, 2], "float32"),
+    "ww": ("sbuf", [P, 2], "float32"),
+    "rt": ("sbuf", [P, 2], "float32"),
+    "rho": ("sbuf", [P, 2], "float32"),
+    "nmu": ("sbuf", [P, 2], "float32"),
+    "yt0": ("sbuf", [P, P], "float32"),
+    "yt1": ("sbuf", [P, P], "float32"),
+    "yo0": ("sbuf", [P, P], "float32"),
+    "yo1": ("sbuf", [P, P], "float32"),
+    "pu0": ("psum", [P, 512], "float32"),
+    "pu1": ("psum", [P, 512], "float32"),
+    "py0": ("psum", [P, 512], "float32"),
+    "py1": ("psum", [P, 512], "float32"),
+}
+SEMAPHORES = ["ld0", "ld1", "cs", "idr", "tp0", "tp1", "r0", "r1", "q", "arr1", "arr2", "sent", "sg", "cv", "scv", "dgv",
+              "n0", "n1", "qs", "tv", "dds", "wv", "nmv", "rts", "rh", "y0", "y1", "m0", "m1", "c0", "c1", "s0", "s1"]
+
+
+def _low_bits(mask, k):
+    out, bit = 0, 1
+    while k > 0 and bit <= mask:
+        if mask & bit:
+            out |= bit
+            k -= 1
+        bit <<= 1
+    return out
+
+
+def _plan(core, T, topo):
+    ranks = list(T.cores)
+
+    def same_chip(a, b):
+        return topo.host(a) == topo.host(b) and topo.chip(a) == topo.chip(b)
+
+    def same_rack(a, b):
+        return topo.rack(topo.host(a)) == topo.rack(topo.host(b))
+
+    def group(c):
+        if RACK_FIRST:
+            return [d for d in ranks if same_rack(c, d)]
+        return [d for d in ranks if same_chip(c, d) or (not same_rack(c, d) and topo.may_write(c, d))]
+
+    order = sorted(ranks, key=lambda c: (ranks.index(group(c)[0]), ranks.index(c)))
+    slot = {c: i for i, c in enumerate(order)}
+    mine = group(core)
+    peers = [d for d in mine if d != core]
+    place = [d for d in ranks if same_chip(core, d)].index(core)
+    partner = [d for d in ranks if d not in mine and topo.may_write(core, d)][place]
+    return slot, peers, partner, min(slot[d] for d in mine)
+
+
+def rank_program(g, core, T, topo):
+    if T.rank_of(core) is None:
+        return
+    A, AX, F = AluOpType, AxisListType, ActivationFunctionType
+    S = T.sem
+    n = len(T.cores)
+    slot, peers, partner, first = _plan(core, T, topo)
+    o = 4 * slot[core]
+    w = 4 * n
+    eng = topo.mask(core, partner)
+    for d in peers:
+        eng &= topo.mask(core, d)
+    eng = _low_bits(eng, NENG)
+    got1 = NENG * len(peers)
+    pu, py = (T.pu0, T.pu1), (T.py0, T.py1)
+
+    g.sync.dma_start(T.xs[0:H, :], T.x[0:H, :]).then_inc(S.ld0, 16)
+    g.scalar.dma_start(T.xs[H:P, :], T.x[H:P, :]).then_inc(S.ld1, 16)
+    g.vector.memset(T.cst[:], 1.0 / P).then_inc(S.cs, 1)
+    g.wait_ge(S.cs, 1)
+    g.affine_select(T.idn[:], T.cst[:], [[-1, P]], A.is_equal, 0.0, 0, 1).then_inc(S.idr, 1)
+
+    g.tensor.wait_ge(S.idr, 1)
+    g.tensor.wait_ge(S.ld0, 16)
+    g.tensor.matmul(pu[0][:, 0:H], T.xs[0:H, 0:P], T.idn[0:H, 0:H], True, True).then_inc(S.tp0, 1)
+    g.tensor.matmul(pu[1][:, 0:H], T.xs[0:H, P:2 * P], T.idn[0:H, 0:H], True, True).then_inc(S.tp1, 1)
+    g.tensor.wait_ge(S.ld1, 16)
+    g.tensor.wait_ge(S.tp0, 1)
+    g.tensor.matmul(pu[0][:, H:P], T.xs[H:P, 0:P], T.idn[H:P, H:P], True, True).then_inc(S.tp0, 1)
+    g.tensor.wait_ge(S.tp1, 1)
+    g.tensor.matmul(pu[1][:, H:P], T.xs[H:P, P:2 * P], T.idn[H:P, H:P], True, True).then_inc(S.tp1, 1)
+
+    g.vector.wait_ge(S.tp0, 2)
+    g.vector.tensor_reduce(T.st[:, o:o + 1], pu[0][:, 0:P], AX.X, A.add, negate=True).then_inc(S.r0, 1)
+    g.vector.wait_ge(S.tp1, 2)
+    g.vector.tensor_reduce(T.st[:, o + 1:o + 2], pu[1][:, 0:P], AX.X, A.add, negate=True).then_inc(S.r1, 1)
+    g.scalar.wait_ge(S.r0, 1)
+    g.scalar.activation(T.j0[:], pu[0][:, 0:P], F.Square, bias=T.st[:, o:o + 1], scale=float(P),
+                        accum_out=T.st[:, o + 2:o + 3]).then_inc(S.q, 1)
+    g.scalar.wait_ge(S.r1, 1)
+    g.scalar.activation(T.j1[:], pu[1][:, 0:P], F.Square, bias=T.st[:, o + 1:o + 2], scale=float(P),
+                        accum_out=T.st[:, o + 3:o + 4]).then_inc(S.q, 1)
+
+    g.wait_ge(S.r0, 1)
+    g.wait_ge(S.r1, 1)
+    g.wait_ge(S.q, 2)
+    ids = []
+    for d in peers:
+        rid, pid = topo.addr(d, core)
+        ids.append(DstId(rid=rid, pnc=pid))
+    g.remote_dma_fused([RemoteDMATransfer(dst_ids=ids, dma_engine_mask=eng, remote_sem=S.arr1, srcs=[T.st[:, o:o + 4]],
+                                          dsts=[T.st[:, o:o + 4] for d in peers], alu_op=0)], local_sem=S.sent)
+    g.wait_ge(S.arr1, got1)
+    rid, pid = topo.addr(partner, core)
+    b = 4 * first
+    g.remote_dma(T.st[:, b:b + 4 * (len(peers) + 1)], T.st[:, b:b + 4 * (len(peers) + 1)], S.arr2, S.sent, pid, rid, eng)
+
+    g.scalar.wait_ge(S.q, 2)
+    g.scalar.activation(T.sig[:], T.st[:, o + 2:o + 4], F.Sqrt, bias=EPS, scale=1.0 / P).then_inc(S.sg, 1)
+    g.vector.wait_ge(S.sg, 1)
+    g.vector.reciprocal(T.cc[:], T.sig[:]).then_inc(S.cv, 1)
+    g.vector.wait_ge(S.cv, 1)
+    g.vector.tensor_tensor(T.sc[:], T.cc[:], T.cc[:], A.mult).then_inc(S.scv, 1)
+    g.vector.wait_ge(S.idr, 1)
+    k = float(P) * float(P) * math.sqrt(float(n) ** 3)
+    g.vector.tensor_scalar(T.dg0[:], T.idn[:], T.cc[:, 0:1], k, A.mult, A.mult).then_inc(S.dgv, 1)
+    g.vector.tensor_scalar(T.dg1[:], T.idn[:], T.cc[:, 1:2], k, A.mult, A.mult).then_inc(S.dgv, 1)
+
+    g.vector.wait_ge(S.r0, 1)
+    g.vector.wait_ge(S.r1, 1)
+    g.vector.wait_ge(S.q, 2)
+    g.vector.wait_ge(S.arr1, got1)
+    g.vector.wait_ge(S.arr2, NENG)
+    g.vector.tensor_reduce(T.nsum[:, 0:1], T.st[:, 0:w:4], AX.X, A.add).then_inc(S.n0, 1)
+    g.vector.tensor_reduce(T.nsum[:, 1:2], T.st[:, 1:w:4], AX.X, A.add).then_inc(S.n1, 1)
+    g.vector.tensor_reduce(T.qsum[:, 0:1], T.st[:, 2:w:4], AX.X, A.add).then_inc(S.qs, 1)
+    g.vector.tensor_reduce(T.qsum[:, 1:2], T.st[:, 3:w:4], AX.X, A.add).then_inc(S.qs, 1)
+    g.vector.wait_ge(S.qs, 2)
+    g.vector.tensor_scalar(T.tq[:], T.qsum[:], float(n * n) / P, float(n) ** 3 * EPS, A.mult, A.add).then_inc(S.tv, 1)
+    g.scalar.wait_ge(S.arr1, got1)
+    g.scalar.wait_ge(S.arr2, NENG)
+    g.scalar.wait_ge(S.n0, 1)
+    g.scalar.activation(T.j2[:], T.st[:, 0:w:4], F.Square, bias=T.nsum[:, 0:1], scale=-float(n),
+                        accum_out=T.dd[:, 0:1]).then_inc(S.dds, 1)
+    g.scalar.wait_ge(S.n1, 1)
+    g.scalar.activation(T.j3[:], T.st[:, 1:w:4], F.Square, bias=T.nsum[:, 1:2], scale=-float(n),
+                        accum_out=T.dd[:, 1:2]).then_inc(S.dds, 1)
+    g.vector.wait_ge(S.tv, 1)
+    g.vector.wait_ge(S.dds, 2)
+    g.vector.tensor_tensor(T.ww[:], T.dd[:], T.tq[:], A.add).then_inc(S.wv, 1)
+    g.vector.wait_ge(S.n0, 1)
+    g.vector.wait_ge(S.n1, 1)
+    g.vector.tensor_scalar(T.nmu[:], T.nsum[:], 1.0 / (n * P), None, A.mult).then_inc(S.nmv, 1)
+    g.scalar.wait_ge(S.scv, 1)
+    g.scalar.wait_ge(S.wv, 1)
+    g.scalar.activation(T.rt[:, 0:1], T.ww[:, 0:1], F.Sqrt, scale=T.sc[:, 0:1]).then_inc(S.rts, 1)
+    g.scalar.activation(T.rt[:, 1:2], T.ww[:, 1:2], F.Sqrt, scale=T.sc[:, 1:2]).then_inc(S.rts, 1)
+    g.vector.wait_ge(S.rts, 2)
+    g.vector.reciprocal(T.rho[:], T.rt[:]).then_inc(S.rh, 1)
+
+    g.vector.wait_ge(S.rh, 1)
+    g.vector.wait_ge(S.nmv, 1)
+    g.vector.tensor_scalar(T.yt0[:], pu[0][:, 0:P], T.nmu[:, 0:1], T.rho[:, 0:1], A.add, A.mult).then_inc(S.y0, 1)
+    g.vector.tensor_scalar(T.yt1[:], pu[1][:, 0:P], T.nmu[:, 1:2], T.rho[:, 1:2], A.add, A.mult).then_inc(S.y1, 1)
+    g.tensor.wait_ge(S.dgv, 2)
+    g.tensor.wait_ge(S.y0, 1)
+    g.tensor.matmul(py[0][:, 0:P], T.yt0[:], T.dg0[:], True, True).then_inc(S.m0, 1)
+    g.tensor.wait_ge(S.y1, 1)
+    g.tensor.matmul(py[1][:, 0:P], T.yt1[:], T.dg1[:], True, True).then_inc(S.m1, 1)
+    g.vector.wait_ge(S.m0, 1)
+    g.vector.tensor_copy(T.yo0[:], py[0][:, 0:P]).then_inc(S.c0, 1)
+    g.scalar.wait_ge(S.m1, 1)
+    g.scalar.activation(T.yo1[:], py[1][:, 0:P], F.Copy).then_inc(S.c1, 1)
+    g.sync.wait_ge(S.c0, 1)
+    g.sync.dma_start(T.y[:, 0:P], T.yo0[:]).then_inc(S.s0, 16)
+    g.scalar.wait_ge(S.c1, 1)
+    g.scalar.dma_start(T.y[:, P:2 * P], T.yo1[:]).then_inc(S.s1, 16)
+    g.sync.wait_ge(S.s0, 16)
+    g.scalar.wait_ge(S.s1, 16)
+    g.wait_ge(S.sent, 2 * NENG)

@@ -11,15 +11,18 @@ RACK_FIRST = True
 SCRATCH = {
     "xs": ("sbuf", [P, 256], "float32"),
     "cst": ("sbuf", [P, P], "float32"),
-    "idn": ("sbuf", [P, P], "float32"),
+    "idn": ("sbuf", [P, P + 4], "float32"),
     "st": ("sbuf", [P, 32], "float32"),
     "j0": ("sbuf", [P, P], "float32"),
     "j1": ("sbuf", [P, P], "float32"),
     "j2": ("sbuf", [P, 8], "float32"),
     "j3": ("sbuf", [P, 8], "float32"),
+    "j4": ("sbuf", [P, 8], "float32"),
     "sig": ("sbuf", [P, 2], "float32"),
     "cc": ("sbuf", [P, 2], "float32"),
     "sc": ("sbuf", [P, 2], "float32"),
+    "dc0": ("sbuf", [P, P], "float32"),
+    "dc1": ("sbuf", [P, P], "float32"),
     "dg0": ("sbuf", [P, P], "float32"),
     "dg1": ("sbuf", [P, P], "float32"),
     "nsum": ("sbuf", [P, 2], "float32"),
@@ -28,19 +31,21 @@ SCRATCH = {
     "dd": ("sbuf", [P, 2], "float32"),
     "ww": ("sbuf", [P, 2], "float32"),
     "rt": ("sbuf", [P, 2], "float32"),
-    "rho": ("sbuf", [P, 2], "float32"),
-    "nmu": ("sbuf", [P, 2], "float32"),
+    "rw": ("sbuf", [P, 2], "float32"),
     "yt0": ("sbuf", [P, P], "float32"),
     "yt1": ("sbuf", [P, P], "float32"),
     "yo0": ("sbuf", [P, P], "float32"),
-    "yo1": ("sbuf", [P, P], "float32"),
+    "yo1": ("sbuf", [P, H], "float32"),
+    "yo2": ("sbuf", [P, H], "float32"),
     "pu0": ("psum", [P, 512], "float32"),
     "pu1": ("psum", [P, 512], "float32"),
     "py0": ("psum", [P, 512], "float32"),
     "py1": ("psum", [P, 512], "float32"),
+    "py2": ("psum", [P, 512], "float32"),
 }
-SEMAPHORES = ["ld0", "ld1", "cs", "idr", "tp0", "tp1", "r0", "r1", "q", "arr1", "arr2", "sent", "sg", "cv", "scv", "dgv",
-              "n0", "n1", "qs", "tv", "dds", "wv", "nmv", "rts", "rh", "y0", "y1", "m0", "m1", "c0", "c1", "s0", "s1"]
+SEMAPHORES = ["ld0", "ld1", "cs", "cs2", "idr", "tp0", "tp1", "r0", "r1", "q0", "q1", "arr1", "arr2", "sent", "sg", "cv",
+              "scv", "dgv", "n0", "n1", "qs0", "qs1", "tv", "dds", "wv", "rwv", "rts", "y0", "y1", "d0", "d1",
+              "m0", "m1", "m2", "c0", "c1", "c2", "s0", "s1", "s2"]
 
 
 def _low_bits(mask, k):
@@ -89,110 +94,128 @@ def rank_program(g, core, T, topo):
     for d in peers:
         eng &= topo.mask(core, d)
     eng = _low_bits(eng, NENG)
-    got1 = NENG * len(peers)
-    pu, py = (T.pu0, T.pu1), (T.py0, T.py1)
+    got1 = 2 * NENG * len(peers)
+    pu = (T.pu0, T.pu1)
 
     g.sync.dma_start(T.xs[0:H, :], T.x[0:H, :]).then_inc(S.ld0, 16)
     g.scalar.dma_start(T.xs[H:P, :], T.x[H:P, :]).then_inc(S.ld1, 16)
-    g.vector.memset(T.cst[:], 1.0 / P).then_inc(S.cs, 1)
+    g.vector.memset(T.cst[:], float(n)).then_inc(S.cs, 1)
+    g.vector.memset(T.idn[:, P:P + 1], -1.0 / P).then_inc(S.cs2, 1)
     g.wait_ge(S.cs, 1)
-    g.affine_select(T.idn[:], T.cst[:], [[-1, P]], A.is_equal, 0.0, 0, 1).then_inc(S.idr, 1)
+    g.affine_select(T.idn[:, 0:P], T.cst[:], [[-1, P]], A.is_equal, 0.0, 0, 1).then_inc(S.idr, 1)
 
     g.tensor.wait_ge(S.idr, 1)
+    g.tensor.wait_ge(S.cs2, 1)
     g.tensor.wait_ge(S.ld0, 16)
-    g.tensor.matmul(pu[0][:, 0:H], T.xs[0:H, 0:P], T.idn[0:H, 0:H], True, True).then_inc(S.tp0, 1)
-    g.tensor.matmul(pu[1][:, 0:H], T.xs[0:H, P:2 * P], T.idn[0:H, 0:H], True, True).then_inc(S.tp1, 1)
     g.tensor.wait_ge(S.ld1, 16)
-    g.tensor.wait_ge(S.tp0, 1)
-    g.tensor.matmul(pu[0][:, H:P], T.xs[H:P, 0:P], T.idn[H:P, H:P], True, True).then_inc(S.tp0, 1)
-    g.tensor.wait_ge(S.tp1, 1)
-    g.tensor.matmul(pu[1][:, H:P], T.xs[H:P, P:2 * P], T.idn[H:P, H:P], True, True).then_inc(S.tp1, 1)
+    g.tensor.matmul(pu[0][:, 0:P + 1], T.xs[:, 0:P], T.idn[:, 0:P + 1], True, True).then_inc(S.tp0, 1)
+    g.tensor.matmul(pu[1][:, 0:P + 1], T.xs[:, P:2 * P], T.idn[:, 0:P + 1], True, True).then_inc(S.tp1, 1)
 
-    g.vector.wait_ge(S.tp0, 2)
-    g.vector.tensor_reduce(T.st[:, o:o + 1], pu[0][:, 0:P], AX.X, A.add, negate=True).then_inc(S.r0, 1)
-    g.vector.wait_ge(S.tp1, 2)
-    g.vector.tensor_reduce(T.st[:, o + 1:o + 2], pu[1][:, 0:P], AX.X, A.add, negate=True).then_inc(S.r1, 1)
+    g.vector.wait_ge(S.tp0, 1)
+    g.vector.tensor_copy(T.st[:, o:o + 1], pu[0][:, P:P + 1]).then_inc(S.r0, 1)
+    g.vector.wait_ge(S.tp1, 1)
+    g.vector.tensor_copy(T.st[:, o + 2:o + 3], pu[1][:, P:P + 1]).then_inc(S.r1, 1)
     g.scalar.wait_ge(S.r0, 1)
-    g.scalar.activation(T.j0[:], pu[0][:, 0:P], F.Square, bias=T.st[:, o:o + 1], scale=float(P),
-                        accum_out=T.st[:, o + 2:o + 3]).then_inc(S.q, 1)
+    g.scalar.activation(T.j0[:], pu[0][:, 0:P], F.Square, bias=T.st[:, o:o + 1], scale=1.0 / n,
+                        accum_out=T.st[:, o + 1:o + 2]).then_inc(S.q0, 1)
     g.scalar.wait_ge(S.r1, 1)
-    g.scalar.activation(T.j1[:], pu[1][:, 0:P], F.Square, bias=T.st[:, o + 1:o + 2], scale=float(P),
-                        accum_out=T.st[:, o + 3:o + 4]).then_inc(S.q, 1)
+    g.scalar.activation(T.j1[:], pu[1][:, 0:P], F.Square, bias=T.st[:, o + 2:o + 3], scale=1.0 / n,
+                        accum_out=T.st[:, o + 3:o + 4]).then_inc(S.q1, 1)
 
-    g.wait_ge(S.r0, 1)
-    g.wait_ge(S.r1, 1)
-    g.wait_ge(S.q, 2)
     ids = []
     for d in peers:
         rid, pid = topo.addr(d, core)
         ids.append(DstId(rid=rid, pnc=pid))
-    g.remote_dma_fused([RemoteDMATransfer(dst_ids=ids, dma_engine_mask=eng, remote_sem=S.arr1, srcs=[T.st[:, o:o + 4]],
-                                          dsts=[T.st[:, o:o + 4] for d in peers], alu_op=0)], local_sem=S.sent)
+
+    def to_peers(lo, hi):
+        g.remote_dma_fused([RemoteDMATransfer(dst_ids=ids, dma_engine_mask=eng, remote_sem=S.arr1, srcs=[T.st[:, lo:hi]],
+                                              dsts=[T.st[:, lo:hi] for d in peers], alu_op=0)], local_sem=S.sent)
+
+    g.wait_ge(S.r0, 1)
+    to_peers(o, o + 1)
+    g.wait_ge(S.q0, 1)
+    g.wait_ge(S.r1, 1)
+    g.wait_ge(S.q1, 1)
+    to_peers(o + 1, o + 4)
     g.wait_ge(S.arr1, got1)
     rid, pid = topo.addr(partner, core)
     b = 4 * first
     g.remote_dma(T.st[:, b:b + 4 * (len(peers) + 1)], T.st[:, b:b + 4 * (len(peers) + 1)], S.arr2, S.sent, pid, rid, eng)
 
-    g.scalar.wait_ge(S.q, 2)
-    g.scalar.activation(T.sig[:], T.st[:, o + 2:o + 4], F.Sqrt, bias=EPS, scale=1.0 / P).then_inc(S.sg, 1)
+    g.scalar.wait_ge(S.q0, 1)
+    g.scalar.wait_ge(S.q1, 1)
+    g.scalar.activation(T.sig[:], T.st[:, o + 1:o + 4:2], F.Sqrt, bias=EPS, scale=1.0 / P).then_inc(S.sg, 1)
     g.vector.wait_ge(S.sg, 1)
     g.vector.reciprocal(T.cc[:], T.sig[:]).then_inc(S.cv, 1)
     g.vector.wait_ge(S.cv, 1)
     g.vector.tensor_tensor(T.sc[:], T.cc[:], T.cc[:], A.mult).then_inc(S.scv, 1)
     g.vector.wait_ge(S.idr, 1)
-    k = float(P) * float(P) * math.sqrt(float(n) ** 3)
-    g.vector.tensor_scalar(T.dg0[:], T.idn[:], T.cc[:, 0:1], k, A.mult, A.mult).then_inc(S.dgv, 1)
-    g.vector.tensor_scalar(T.dg1[:], T.idn[:], T.cc[:, 1:2], k, A.mult, A.mult).then_inc(S.dgv, 1)
+    k = math.sqrt(float(n) ** 3) / float(n * n)
+    g.vector.tensor_scalar(T.dc0[:], T.idn[:, 0:P], T.sig[:, 0:1], k, A.mult, A.mult).then_inc(S.dgv, 1)
+    g.vector.tensor_scalar(T.dc1[:], T.idn[:, 0:P], T.sig[:, 1:2], k, A.mult, A.mult).then_inc(S.dgv, 1)
 
     g.vector.wait_ge(S.r0, 1)
     g.vector.wait_ge(S.r1, 1)
-    g.vector.wait_ge(S.q, 2)
+    g.vector.wait_ge(S.q0, 1)
+    g.vector.wait_ge(S.q1, 1)
     g.vector.wait_ge(S.arr1, got1)
     g.vector.wait_ge(S.arr2, NENG)
     g.vector.tensor_reduce(T.nsum[:, 0:1], T.st[:, 0:w:4], AX.X, A.add).then_inc(S.n0, 1)
-    g.vector.tensor_reduce(T.nsum[:, 1:2], T.st[:, 1:w:4], AX.X, A.add).then_inc(S.n1, 1)
-    g.vector.tensor_reduce(T.qsum[:, 0:1], T.st[:, 2:w:4], AX.X, A.add).then_inc(S.qs, 1)
-    g.vector.tensor_reduce(T.qsum[:, 1:2], T.st[:, 3:w:4], AX.X, A.add).then_inc(S.qs, 1)
-    g.vector.wait_ge(S.qs, 2)
-    g.vector.tensor_scalar(T.tq[:], T.qsum[:], float(n * n) / P, float(n) ** 3 * EPS, A.mult, A.add).then_inc(S.tv, 1)
+    g.vector.tensor_reduce(T.nsum[:, 1:2], T.st[:, 2:w:4], AX.X, A.add).then_inc(S.n1, 1)
+    g.vector.tensor_reduce(T.qsum[:, 1:2], T.st[:, 3:w:4], AX.X, A.add).then_inc(S.qs1, 1)
+    g.scalar.wait_ge(S.r0, 1)
+    g.scalar.wait_ge(S.r1, 1)
     g.scalar.wait_ge(S.arr1, got1)
     g.scalar.wait_ge(S.arr2, NENG)
+    g.scalar.activation(T.j4[:], T.st[:, 1:w:4], F.Copy, accum_out=T.qsum[:, 0:1]).then_inc(S.qs0, 1)
     g.scalar.wait_ge(S.n0, 1)
     g.scalar.activation(T.j2[:], T.st[:, 0:w:4], F.Square, bias=T.nsum[:, 0:1], scale=-float(n),
                         accum_out=T.dd[:, 0:1]).then_inc(S.dds, 1)
     g.scalar.wait_ge(S.n1, 1)
-    g.scalar.activation(T.j3[:], T.st[:, 1:w:4], F.Square, bias=T.nsum[:, 1:2], scale=-float(n),
+    g.scalar.activation(T.j3[:], T.st[:, 2:w:4], F.Square, bias=T.nsum[:, 1:2], scale=-float(n),
                         accum_out=T.dd[:, 1:2]).then_inc(S.dds, 1)
+    g.vector.wait_ge(S.qs0, 1)
+    g.vector.wait_ge(S.qs1, 1)
+    g.vector.tensor_scalar(T.tq[:], T.qsum[:], float(n * n) / P, float(n) ** 3 * EPS, A.mult, A.add).then_inc(S.tv, 1)
     g.vector.wait_ge(S.tv, 1)
     g.vector.wait_ge(S.dds, 2)
     g.vector.tensor_tensor(T.ww[:], T.dd[:], T.tq[:], A.add).then_inc(S.wv, 1)
-    g.vector.wait_ge(S.n0, 1)
-    g.vector.wait_ge(S.n1, 1)
-    g.vector.tensor_scalar(T.nmu[:], T.nsum[:], 1.0 / (n * P), None, A.mult).then_inc(S.nmv, 1)
+    g.vector.wait_ge(S.wv, 1)
+    g.vector.reciprocal(T.rw[:], T.ww[:]).then_inc(S.rwv, 1)
     g.scalar.wait_ge(S.scv, 1)
     g.scalar.wait_ge(S.wv, 1)
     g.scalar.activation(T.rt[:, 0:1], T.ww[:, 0:1], F.Sqrt, scale=T.sc[:, 0:1]).then_inc(S.rts, 1)
     g.scalar.activation(T.rt[:, 1:2], T.ww[:, 1:2], F.Sqrt, scale=T.sc[:, 1:2]).then_inc(S.rts, 1)
-    g.vector.wait_ge(S.rts, 2)
-    g.vector.reciprocal(T.rho[:], T.rt[:]).then_inc(S.rh, 1)
 
-    g.vector.wait_ge(S.rh, 1)
-    g.vector.wait_ge(S.nmv, 1)
-    g.vector.tensor_scalar(T.yt0[:], pu[0][:, 0:P], T.nmu[:, 0:1], T.rho[:, 0:1], A.add, A.mult).then_inc(S.y0, 1)
-    g.vector.tensor_scalar(T.yt1[:], pu[1][:, 0:P], T.nmu[:, 1:2], T.rho[:, 1:2], A.add, A.mult).then_inc(S.y1, 1)
-    g.tensor.wait_ge(S.dgv, 2)
+    g.vector.wait_ge(S.n0, 1)
+    g.vector.wait_ge(S.n1, 1)
+    g.vector.wait_ge(S.rts, 2)
+    g.vector.tensor_scalar(T.yt0[:], pu[0][:, 0:P], T.nsum[:, 0:1], T.rt[:, 0:1], A.add, A.mult).then_inc(S.y0, 1)
+    g.vector.tensor_scalar(T.yt1[:], pu[1][:, 0:P], T.nsum[:, 1:2], T.rt[:, 1:2], A.add, A.mult).then_inc(S.y1, 1)
+    g.scalar.wait_ge(S.dgv, 2)
+    g.scalar.wait_ge(S.rwv, 1)
+    g.scalar.activation(T.dg0[:], T.dc0[:], F.Identity, scale=T.rw[:, 0:1]).then_inc(S.d0, 1)
+    g.scalar.activation(T.dg1[:], T.dc1[:], F.Identity, scale=T.rw[:, 1:2]).then_inc(S.d1, 1)
     g.tensor.wait_ge(S.y0, 1)
-    g.tensor.matmul(py[0][:, 0:P], T.yt0[:], T.dg0[:], True, True).then_inc(S.m0, 1)
+    g.tensor.wait_ge(S.d0, 1)
+    g.tensor.matmul(T.py0[:, 0:P], T.yt0[:], T.dg0[:], True, True).then_inc(S.m0, 1)
     g.tensor.wait_ge(S.y1, 1)
-    g.tensor.matmul(py[1][:, 0:P], T.yt1[:], T.dg1[:], True, True).then_inc(S.m1, 1)
+    g.tensor.wait_ge(S.d1, 1)
+    g.tensor.matmul(T.py1[:, 0:H], T.yt1[0:H, :], T.dg1[0:H, 0:H], True, True).then_inc(S.m1, 1)
+    g.tensor.matmul(T.py2[:, 0:H], T.yt1[H:P, :], T.dg1[H:P, H:P], True, True).then_inc(S.m2, 1)
     g.vector.wait_ge(S.m0, 1)
-    g.vector.tensor_copy(T.yo0[:], py[0][:, 0:P]).then_inc(S.c0, 1)
+    g.vector.tensor_copy(T.yo0[:], T.py0[:, 0:P]).then_inc(S.c0, 1)
     g.scalar.wait_ge(S.m1, 1)
-    g.scalar.activation(T.yo1[:], py[1][:, 0:P], F.Copy).then_inc(S.c1, 1)
+    g.scalar.activation(T.yo1[:], T.py1[:, 0:H], F.Copy).then_inc(S.c1, 1)
+    g.vector.wait_ge(S.m2, 1)
+    g.vector.tensor_copy(T.yo2[:], T.py2[:, 0:H]).then_inc(S.c2, 1)
     g.sync.wait_ge(S.c0, 1)
     g.sync.dma_start(T.y[:, 0:P], T.yo0[:]).then_inc(S.s0, 16)
     g.scalar.wait_ge(S.c1, 1)
-    g.scalar.dma_start(T.y[:, P:2 * P], T.yo1[:]).then_inc(S.s1, 16)
+    g.scalar.dma_start(T.y[:, P:P + H], T.yo1[:]).then_inc(S.s1, 16)
+    g.sync.wait_ge(S.c2, 1)
+    g.sync.dma_start(T.y[:, P + H:2 * P], T.yo2[:]).then_inc(S.s2, 16)
     g.sync.wait_ge(S.s0, 16)
+    g.sync.wait_ge(S.s2, 16)
     g.scalar.wait_ge(S.s1, 16)
-    g.wait_ge(S.sent, 2 * NENG)
+    g.wait_ge(S.sent, 3 * NENG)

import math
from concourse.bass import DstId, RemoteDMATransfer
from concourse.mybir import AluOpType, AxisListType, ActivationFunctionType

P = 128
H = 64
EPS = 0.01
NENG = 8
RACK_FIRST = True

SCRATCH = {
    "xs": ("sbuf", [P, 256], "float32"),
    "cst": ("sbuf", [P, P], "float32"),
    "idn": ("sbuf", [P, P + 4], "float32"),
    "st": ("sbuf", [P, 32], "float32"),
    "j0": ("sbuf", [P, P], "float32"),
    "j1": ("sbuf", [P, P], "float32"),
    "j2": ("sbuf", [P, 8], "float32"),
    "j3": ("sbuf", [P, 8], "float32"),
    "j4": ("sbuf", [P, 8], "float32"),
    "sig": ("sbuf", [P, 2], "float32"),
    "cc": ("sbuf", [P, 2], "float32"),
    "sc": ("sbuf", [P, 2], "float32"),
    "dc0": ("sbuf", [P, P], "float32"),
    "dc1": ("sbuf", [P, P], "float32"),
    "dg0": ("sbuf", [P, P], "float32"),
    "dg1": ("sbuf", [P, P], "float32"),
    "nsum": ("sbuf", [P, 2], "float32"),
    "qsum": ("sbuf", [P, 2], "float32"),
    "tq": ("sbuf", [P, 2], "float32"),
    "dd": ("sbuf", [P, 2], "float32"),
    "ww": ("sbuf", [P, 2], "float32"),
    "rt": ("sbuf", [P, 2], "float32"),
    "rw": ("sbuf", [P, 2], "float32"),
    "yt0": ("sbuf", [P, P], "float32"),
    "yt1": ("sbuf", [P, P], "float32"),
    "yo0": ("sbuf", [P, P], "float32"),
    "yo1": ("sbuf", [P, H], "float32"),
    "yo2": ("sbuf", [P, H], "float32"),
    "pu0": ("psum", [P, 512], "float32"),
    "pu1": ("psum", [P, 512], "float32"),
    "py0": ("psum", [P, 512], "float32"),
    "py1": ("psum", [P, 512], "float32"),
    "py2": ("psum", [P, 512], "float32"),
}
SEMAPHORES = ["ld0", "ld1", "cs", "cs2", "idr", "tp0", "tp1", "r0", "r1", "q0", "q1", "arr1", "arr2", "sent", "sg", "cv",
              "scv", "dgv", "n0", "n1", "qs0", "qs1", "tv", "dds", "wv", "rwv", "rts", "y0", "y1", "d0", "d1",
              "m0", "m1", "m2", "c0", "c1", "c2", "s0", "s1", "s2"]


def _low_bits(mask, k):
    out, bit = 0, 1
    while k > 0 and bit <= mask:
        if mask & bit:
            out |= bit
            k -= 1
        bit <<= 1
    return out


def _plan(core, T, topo):
    ranks = list(T.cores)

    def same_chip(a, b):
        return topo.host(a) == topo.host(b) and topo.chip(a) == topo.chip(b)

    def same_rack(a, b):
        return topo.rack(topo.host(a)) == topo.rack(topo.host(b))

    def group(c):
        if RACK_FIRST:
            return [d for d in ranks if same_rack(c, d)]
        return [d for d in ranks if same_chip(c, d) or (not same_rack(c, d) and topo.may_write(c, d))]

    order = sorted(ranks, key=lambda c: (ranks.index(group(c)[0]), ranks.index(c)))
    slot = {c: i for i, c in enumerate(order)}
    mine = group(core)
    peers = [d for d in mine if d != core]
    place = [d for d in ranks if same_chip(core, d)].index(core)
    partner = [d for d in ranks if d not in mine and topo.may_write(core, d)][place]
    return slot, peers, partner, min(slot[d] for d in mine)


def rank_program(g, core, T, topo):
    if T.rank_of(core) is None:
        return
    A, AX, F = AluOpType, AxisListType, ActivationFunctionType
    S = T.sem
    n = len(T.cores)
    slot, peers, partner, first = _plan(core, T, topo)
    o = 4 * slot[core]
    w = 4 * n
    eng = topo.mask(core, partner)
    for d in peers:
        eng &= topo.mask(core, d)
    eng = _low_bits(eng, NENG)
    got1 = 2 * NENG * len(peers)
    pu = (T.pu0, T.pu1)

    g.sync.dma_start(T.xs[0:H, :], T.x[0:H, :]).then_inc(S.ld0, 16)
    g.scalar.dma_start(T.xs[H:P, :], T.x[H:P, :]).then_inc(S.ld1, 16)
    g.vector.memset(T.cst[:], float(n)).then_inc(S.cs, 1)
    g.vector.memset(T.idn[:, P:P + 1], -1.0 / P).then_inc(S.cs2, 1)
    g.wait_ge(S.cs, 1)
    g.affine_select(T.idn[:, 0:P], T.cst[:], [[-1, P]], A.is_equal, 0.0, 0, 1).then_inc(S.idr, 1)

    g.tensor.wait_ge(S.idr, 1)
    g.tensor.wait_ge(S.cs2, 1)
    g.tensor.wait_ge(S.ld0, 16)
    g.tensor.wait_ge(S.ld1, 16)
    g.tensor.matmul(pu[0][:, 0:P + 1], T.xs[:, 0:P], T.idn[:, 0:P + 1], True, True).then_inc(S.tp0, 1)
    g.tensor.matmul(pu[1][:, 0:P + 1], T.xs[:, P:2 * P], T.idn[:, 0:P + 1], True, True).then_inc(S.tp1, 1)

    g.vector.wait_ge(S.tp0, 1)
    g.vector.tensor_copy(T.st[:, o:o + 1], pu[0][:, P:P + 1]).then_inc(S.r0, 1)
    g.vector.wait_ge(S.tp1, 1)
    g.vector.tensor_copy(T.st[:, o + 2:o + 3], pu[1][:, P:P + 1]).then_inc(S.r1, 1)
    g.scalar.wait_ge(S.r0, 1)
    g.scalar.activation(T.j0[:], pu[0][:, 0:P], F.Square, bias=T.st[:, o:o + 1], scale=1.0 / n,
                        accum_out=T.st[:, o + 1:o + 2]).then_inc(S.q0, 1)
    g.scalar.wait_ge(S.r1, 1)
    g.scalar.activation(T.j1[:], pu[1][:, 0:P], F.Square, bias=T.st[:, o + 2:o + 3], scale=1.0 / n,
                        accum_out=T.st[:, o + 3:o + 4]).then_inc(S.q1, 1)

    ids = []
    for d in peers:
        rid, pid = topo.addr(d, core)
        ids.append(DstId(rid=rid, pnc=pid))

    def to_peers(lo, hi):
        g.remote_dma_fused([RemoteDMATransfer(dst_ids=ids, dma_engine_mask=eng, remote_sem=S.arr1, srcs=[T.st[:, lo:hi]],
                                              dsts=[T.st[:, lo:hi] for d in peers], alu_op=0)], local_sem=S.sent)

    g.wait_ge(S.r0, 1)
    to_peers(o, o + 1)
    g.wait_ge(S.q0, 1)
    g.wait_ge(S.r1, 1)
    g.wait_ge(S.q1, 1)
    to_peers(o + 1, o + 4)
    g.wait_ge(S.arr1, got1)
    rid, pid = topo.addr(partner, core)
    b = 4 * first
    g.remote_dma(T.st[:, b:b + 4 * (len(peers) + 1)], T.st[:, b:b + 4 * (len(peers) + 1)], S.arr2, S.sent, pid, rid, eng)

    g.scalar.wait_ge(S.q0, 1)
    g.scalar.wait_ge(S.q1, 1)
    g.scalar.activation(T.sig[:], T.st[:, o + 1:o + 4:2], F.Sqrt, bias=EPS, scale=1.0 / P).then_inc(S.sg, 1)
    g.vector.wait_ge(S.sg, 1)
    g.vector.reciprocal(T.cc[:], T.sig[:]).then_inc(S.cv, 1)
    g.vector.wait_ge(S.cv, 1)
    g.vector.tensor_tensor(T.sc[:], T.cc[:], T.cc[:], A.mult).then_inc(S.scv, 1)
    g.vector.wait_ge(S.idr, 1)
    k = math.sqrt(float(n) ** 3) / float(n * n)
    g.vector.tensor_scalar(T.dc0[:], T.idn[:, 0:P], T.sig[:, 0:1], k, A.mult, A.mult).then_inc(S.dgv, 1)
    g.vector.tensor_scalar(T.dc1[:], T.idn[:, 0:P], T.sig[:, 1:2], k, A.mult, A.mult).then_inc(S.dgv, 1)

    g.vector.wait_ge(S.r0, 1)
    g.vector.wait_ge(S.r1, 1)
    g.vector.wait_ge(S.q0, 1)
    g.vector.wait_ge(S.q1, 1)
    g.vector.wait_ge(S.arr1, got1)
    g.vector.wait_ge(S.arr2, NENG)
    g.vector.tensor_reduce(T.nsum[:, 0:1], T.st[:, 0:w:4], AX.X, A.add).then_inc(S.n0, 1)
    g.vector.tensor_reduce(T.nsum[:, 1:2], T.st[:, 2:w:4], AX.X, A.add).then_inc(S.n1, 1)
    g.vector.tensor_reduce(T.qsum[:, 1:2], T.st[:, 3:w:4], AX.X, A.add).then_inc(S.qs1, 1)
    g.scalar.wait_ge(S.r0, 1)
    g.scalar.wait_ge(S.r1, 1)
    g.scalar.wait_ge(S.arr1, got1)
    g.scalar.wait_ge(S.arr2, NENG)
    g.scalar.activation(T.j4[:], T.st[:, 1:w:4], F.Copy, accum_out=T.qsum[:, 0:1]).then_inc(S.qs0, 1)
    g.scalar.wait_ge(S.n0, 1)
    g.scalar.activation(T.j2[:], T.st[:, 0:w:4], F.Square, bias=T.nsum[:, 0:1], scale=-float(n),
                        accum_out=T.dd[:, 0:1]).then_inc(S.dds, 1)
    g.scalar.wait_ge(S.n1, 1)
    g.scalar.activation(T.j3[:], T.st[:, 2:w:4], F.Square, bias=T.nsum[:, 1:2], scale=-float(n),
                        accum_out=T.dd[:, 1:2]).then_inc(S.dds, 1)
    g.vector.wait_ge(S.qs0, 1)
    g.vector.wait_ge(S.qs1, 1)
    g.vector.tensor_scalar(T.tq[:], T.qsum[:], float(n * n) / P, float(n) ** 3 * EPS, A.mult, A.add).then_inc(S.tv, 1)
    g.vector.wait_ge(S.tv, 1)
    g.vector.wait_ge(S.dds, 2)
    g.vector.tensor_tensor(T.ww[:], T.dd[:], T.tq[:], A.add).then_inc(S.wv, 1)
    g.vector.wait_ge(S.wv, 1)
    g.vector.reciprocal(T.rw[:], T.ww[:]).then_inc(S.rwv, 1)
    g.scalar.wait_ge(S.scv, 1)
    g.scalar.wait_ge(S.wv, 1)
    g.scalar.activation(T.rt[:, 0:1], T.ww[:, 0:1], F.Sqrt, scale=T.sc[:, 0:1]).then_inc(S.rts, 1)
    g.scalar.activation(T.rt[:, 1:2], T.ww[:, 1:2], F.Sqrt, scale=T.sc[:, 1:2]).then_inc(S.rts, 1)

    g.vector.wait_ge(S.n0, 1)
    g.vector.wait_ge(S.n1, 1)
    g.vector.wait_ge(S.rts, 2)
    g.vector.tensor_scalar(T.yt0[:], pu[0][:, 0:P], T.nsum[:, 0:1], T.rt[:, 0:1], A.add, A.mult).then_inc(S.y0, 1)
    g.vector.tensor_scalar(T.yt1[:], pu[1][:, 0:P], T.nsum[:, 1:2], T.rt[:, 1:2], A.add, A.mult).then_inc(S.y1, 1)
    g.scalar.wait_ge(S.dgv, 2)
    g.scalar.wait_ge(S.rwv, 1)
    g.scalar.activation(T.dg0[:], T.dc0[:], F.Identity, scale=T.rw[:, 0:1]).then_inc(S.d0, 1)
    g.scalar.activation(T.dg1[:], T.dc1[:], F.Identity, scale=T.rw[:, 1:2]).then_inc(S.d1, 1)
    g.tensor.wait_ge(S.y0, 1)
    g.tensor.wait_ge(S.d0, 1)
    g.tensor.matmul(T.py0[:, 0:P], T.yt0[:], T.dg0[:], True, True).then_inc(S.m0, 1)
    g.tensor.wait_ge(S.y1, 1)
    g.tensor.wait_ge(S.d1, 1)
    g.tensor.matmul(T.py1[:, 0:H], T.yt1[0:H, :], T.dg1[0:H, 0:H], True, True).then_inc(S.m1, 1)
    g.tensor.matmul(T.py2[:, 0:H], T.yt1[H:P, :], T.dg1[H:P, H:P], True, True).then_inc(S.m2, 1)
    g.vector.wait_ge(S.m0, 1)
    g.vector.tensor_copy(T.yo0[:], T.py0[:, 0:P]).then_inc(S.c0, 1)
    g.scalar.wait_ge(S.m1, 1)
    g.scalar.activation(T.yo1[:], T.py1[:, 0:H], F.Copy).then_inc(S.c1, 1)
    g.vector.wait_ge(S.m2, 1)
    g.vector.tensor_copy(T.yo2[:], T.py2[:, 0:H]).then_inc(S.c2, 1)
    g.sync.wait_ge(S.c0, 1)
    g.sync.dma_start(T.y[:, 0:P], T.yo0[:]).then_inc(S.s0, 16)
    g.scalar.wait_ge(S.c1, 1)
    g.scalar.dma_start(T.y[:, P:P + H], T.yo1[:]).then_inc(S.s1, 16)
    g.sync.wait_ge(S.c2, 1)
    g.sync.dma_start(T.y[:, P + H:2 * P], T.yo2[:]).then_inc(S.s2, 16)
    g.sync.wait_ge(S.s0, 16)
    g.sync.wait_ge(S.s2, 16)
    g.scalar.wait_ge(S.s1, 16)
    g.wait_ge(S.sent, 3 * NENG)
